import numpy as np
import ml_dtypes


def mxq(x, axis, fmt="e4m3"):
    dtype, down = {"e4m3": (ml_dtypes.float8_e4m3fn, 7), "e5m2": (ml_dtypes.float8_e5m2, 14)}[fmt]
    v = np.moveaxis(np.asarray(x, np.float32).astype(ml_dtypes.bfloat16).astype(np.float64), axis, -1)
    blocks = v.reshape(v.shape[:-1] + (-1, 32))
    amax = np.abs(blocks).max(-1, keepdims=True)
    byte = np.maximum(np.where(amax > 0, np.frexp(amax)[1] - 1 + 127, 0) - down, 1)
    scale = np.exp2(byte - 127.0)
    codes = (blocks / scale).astype(np.float32).astype(dtype).astype(np.float64)
    return np.moveaxis((codes * scale).reshape(v.shape), -1, axis)


WIDE = False


def mx_kscale(k):
    if not WIDE:
        return np.ones(k)
    levels = np.array([10, -10, 5, -5, 0])
    if k % 512:
        return np.exp2(np.random.permutation(np.resize(levels, k // 32))).repeat(32)
    a = np.empty((k // 512, 16))
    for p in range(k // 512):
        a[p, :8] = np.random.permutation(np.resize(levels, 8))
        for g in range(8):
            far = levels[np.abs(levels - a[p, g]) >= 10]
            a[p, g + 8] = far[np.random.randint(len(far))]
    return np.exp2(a.ravel()).repeat(32)


def f64(x):
    return np.asarray(x).astype(np.float64)


def striped(idx):
    return np.tile(np.asarray(idx).reshape(-1, 16).T, (8, 1)).astype(np.uint16)


def unstriped(offs):
    return offs[:16].T.reshape(-1).astype(np.int64)


E2M1 = np.array([0.0, 0.5, 1.0, 1.5, 2.0, 3.0, 4.0, 6.0, -0.0, -0.5, -1.0, -1.5, -2.0, -3.0, -4.0, -6.0])


def pack_weight(w, fmt):
    k, n = w.shape
    w = f64(np.asarray(w, np.float32).astype(ml_dtypes.bfloat16)).reshape(k // 32, 32, n)
    amax = np.abs(w).max(1)
    if fmt == "e4m3":
        byte = np.frexp(amax)[1] - 1 + 127 - 7
    else:
        mant, ex = np.frexp(amax / 6.0)
        byte = np.where(mant > 0.5, ex, ex - 1) + 127
    byte = np.clip(np.where(amax > 0, byte, 1), 1, 254)
    scaled = (w * np.exp2(127.0 - byte)[:, None, :]).reshape(k, n).astype(np.float32)
    by_word = np.ascontiguousarray(scaled.reshape(k // 512, 128, 4, n).transpose(0, 1, 3, 2))
    if fmt == "e4m3":
        words = by_word.astype(ml_dtypes.float8_e4m3fn).view(np.uint8)
    else:
        c = by_word.astype(ml_dtypes.float4_e2m1fn).view(np.uint8) & 0xF
        words = (c[..., 0::2] | (c[..., 1::2] << 4)).reshape(k // 512, 128, 2 * n)
    return np.ascontiguousarray(words), np.ascontiguousarray(byte.astype(np.uint8).reshape(k // 512, 16, n))


def unpack_weight(words, scales, fmt):
    g, _, n = scales.shape
    words = np.ascontiguousarray(words).reshape(g, 128, n, -1)
    if fmt == "e4m3":
        vals = words.view(ml_dtypes.float8_e4m3fn).astype(np.float64)
    else:
        nib = np.empty((g, 128, n, 4), np.uint8)
        nib[..., 0::2] = words & 0xF
        nib[..., 1::2] = words >> 4
        vals = E2M1[nib]
    vals = vals * np.repeat(np.exp2(scales.astype(np.float64) - 127.0), 8, axis=1)[..., None]
    return vals.transpose(0, 1, 3, 2).reshape(g * 512, n)


def bf(x):
    return np.asarray(x, np.float32).astype(ml_dtypes.bfloat16)


def planes(Y):
    r, m = Y.shape
    b = f64(bf(Y)).reshape(r // 32, 32, m)
    amax = np.abs(b).max(1)
    byte = np.clip(np.where(amax > 0, np.frexp(amax)[1] - 1 + 127 - 7, 1), 1, 254)
    codes = (b * np.exp2(127.0 - byte)[:, None, :]).reshape(r, m).astype(np.float32).astype(ml_dtypes.float8_e4m3fn).view(np.uint8)
    words = codes.reshape(r // 512, 128, 4, m).transpose(0, 1, 3, 2)
    return np.ascontiguousarray(words), np.ascontiguousarray(byte.astype(np.uint8).reshape(r // 512, 16, m))


D, E, T, I, Q, G = 512, 512, 2048, 512, 256, 64


def setup_inputs():
    n = np.random.standard_normal
    idx = np.random.permutation(T)[:I]
    fd = mx_kscale(D)
    fi = mx_kscale(I)
    ti = np.ones(T)
    ti[idx] = fi
    keysp = pack_weight(n((D, T)) / fd[:, None], "e4m3")
    return {
        "query": (n((D, Q)) * 0.8 / np.sqrt(D) * fd[:, None]).astype(np.float32),
        "query2": (n((D, Q)) * 0.8 / np.sqrt(D) * fd[:, None]).astype(np.float32),
        "keys_words": keysp[0],
        "keys_scales": keysp[1],
        "os": (np.random.uniform(4.0, 16.0, (1, I)) * fi).astype(np.float32),
        "vals": (n((E, T)) / ti).astype(np.float32),
        "offs": striped(idx),
    }


def reference(query, query2, keys_words, keys_scales, os, vals, offs):
    idx = unstriped(offs)
    keysu = unpack_weight(keys_words, keys_scales, "e4m3")
    queryq = mxq(f64(query), 0, "e4m3")
    keysidxg = keysu[:, idx]
    a = queryq.T @ keysidxg
    query2q = mxq(f64(query2), 0, "e4m3")
    b = query2q.T @ keysidxg
    pa = np.exp(a)
    sa = pa.reshape(Q, G, I // G).sum(axis=2)
    z = np.sum(sa, axis=1, keepdims=True)
    pb = np.exp(b)
    sb = pb.reshape(Q, G, I // G).sum(axis=2)
    r = sa / z / sb
    rr = np.repeat(r, I // G, axis=1)
    w = pb * rr
    wo1 = w * f64(os)
    wt1 = wo1.T
    vt1 = f64(vals)[:, idx].T
    vt1q = mxq(vt1, 0, "e4m3")
    wt1q = mxq(wt1, 0, "e4m3")
    o = vt1q.T @ wt1q
    words, scales = planes(o)
    return o, words, scales

@@ -1,0 +1,255 @@
+from contextlib import ExitStack
+
+import concourse.mybir as mybir
+from concourse.masks import make_identity
+
+D, E, T, I, Q, G = 512, 512, 2048, 512, 256, 64
+FLOPS = 2 * (2 * D * Q * I) + 2 * I * E * Q
+
+F32 = mybir.dt.float32
+BF16 = mybir.dt.bfloat16
+I32 = mybir.dt.int32
+U32 = mybir.dt.uint32
+U16 = mybir.dt.uint16
+U8 = mybir.dt.uint8
+FP8X4 = mybir.dt.float8_e4m3fn_x4
+ALU = mybir.AluOpType
+ACT = mybir.ActivationFunctionType
+AX = mybir.AxisListType
+
+P = 128
+PACK = 4
+PAGE = I // G
+HALVES = Q // P
+
+
+def tile_attend_pagethensecond_pl_kernel(
+    tc, query, query2, keys_words, keys_scales, slot_factor, vals, offs, out_0, out_1, out_2
+):
+    nc = tc.nc
+    with ExitStack() as ctx:
+        keep = ctx.enter_context(tc.tile_pool(name="keep", bufs=1))
+        reuse = ctx.enter_context(tc.tile_pool(name="reuse", bufs=1))
+        psum = ctx.enter_context(tc.psum_pool(name="psum", bufs=1))
+
+        def sb(shape, dtype, name, tag=None):
+            return keep.tile(shape, dtype, name=name, tag=tag or name, align_bytes=64)
+
+        banks = [psum.tile([P, I], F32, name="bank_%d" % n) for n in range(8)]
+
+        offsets = keep.tile([P, I // 16], U16, name="offsets")
+        nc.sync.dma_start(offsets[:], offs)
+        factor = sb([P, PACK], F32, "factor")
+        nc.scalar.dma_start(factor[:], slot_factor.rearrange("o (p j) -> (o p) j", j=PACK))
+        key_bytes = sb([P, T], U8, "key_bytes")
+        nc.vector.memset(key_bytes[:].bitcast(I32), 0)
+        raw_q = {name: sb([P, PACK, Q], F32, "raw_q_" + name) for name in ("b", "a")}
+        nc.sync.dma_start(raw_q["b"][:], query2.rearrange("(p j) w -> p j w", j=PACK))
+        for quad in range(4):
+            nc.sync.dma_start(
+                key_bytes[32 * quad : 32 * quad + 4, :].bitcast(I32),
+                keys_scales[0, 4 * quad : 4 * quad + 4, :].bitcast(I32),
+            )
+        key_words = sb([P, T], U32, "key_words")
+        nc.sync.dma_start(
+            key_words[:].bitcast(I32),
+            keys_words[0].rearrange("p n t -> p (n t)").bitcast(I32),
+        )
+        nc.sync.dma_start(raw_q["a"][:], query.rearrange("(p j) w -> p j w", j=PACK))
+        pool_rows = vals.rearrange("(p j) c -> p j c", j=PACK)
+        windows = []
+        for t in range(PACK):
+            if t < PACK - 1:
+                window = sb([P, T], F32, "vals_%d" % t)
+            else:
+                window = reuse.tile([P, T], F32, name="vals_last", offset=0, align_bytes=64)
+            nc.sync.dma_start(window[:], pool_rows[:, t, :])
+            windows.append(window)
+
+        ident = sb([P, P], F32, "ident")
+        make_identity(nc, ident[:])
+
+        spread = banks[4][:].rearrange("p (j n) -> p j n", j=PACK)
+        for j in range(PACK):
+            nc.tensor.transpose(spread[:, j, :], factor[:, j : j + 1].to_broadcast([P, P]), ident[:])
+
+        k_scales = sb([P, I], U8, "k_scales")
+        nc.vector.tensor_copy(k_scales[:], key_bytes[:].indirect(offsets[:]))
+        k_codes = sb([P, I], U32, "k_codes")
+        nc.vector.tensor_copy(k_codes[:], key_words[:].indirect(offsets[:]))
+
+        prob_b = [sb([P, I], F32, "prob_b_%d" % h) for h in range(HALVES)]
+        prob_a = sb([P, PAGE, HALVES, G], F32, "prob_a")
+        row_sum = sb([P, HALVES], F32, "row_sum")
+        for n, name in enumerate(("b", "a")):
+            grouped = sb([P, Q, PACK], BF16, "q_grouped_" + name)
+            nc.vector.tensor_copy(
+                grouped[:].rearrange("p (c i) t -> p c t i", i=4),
+                raw_q[name][:].rearrange("p t (c i) -> p c t i", i=4),
+            )
+            q_codes = sb([P, Q], U32, "q_codes_" + name)
+            q_scales = sb([P, Q], U8, "q_scales_" + name)
+            nc.vector.quantize_mx(
+                q_codes[:].bitcast(FP8X4), q_scales[:], grouped[:].rearrange("p w t -> p (w t)")
+            )
+            for h in range(HALVES):
+                cols = slice(h * P, (h + 1) * P)
+                scores = banks[HALVES * n + h]
+                nc.tensor.matmul_mx(
+                    scores[:],
+                    lhsT=q_codes[:, cols].bitcast(FP8X4),
+                    lhsT_scale=q_scales[:, cols],
+                    rhs=k_codes[:].bitcast(FP8X4),
+                    rhs_scale=k_scales[:],
+                    start=True,
+                    stop=True,
+                )
+                if name == "a":
+                    nc.scalar.activation(
+                        prob_a[:, :, h, :],
+                        scores[:].rearrange("p (g c) -> p c g", c=PAGE),
+                        ACT.Exp,
+                        accum_out=row_sum[:, h : h + 1],
+                    )
+                else:
+                    nc.scalar.activation(prob_b[h][:], scores[:], ACT.Exp)
+
+        page_b = sb([P, HALVES, G], F32, "page_b")
+        inv_b = sb([P, HALVES, G], F32, "inv_b")
+        scaled = sb([P, HALVES, I], F32, "scaled", tag="raw_q_a")
+        for h in range(HALVES):
+            nc.vector.tensor_reduce(
+                page_b[:, h, :], prob_b[h][:].rearrange("p (g c) -> p g c", c=PAGE), AX.X, ALU.add
+            )
+            nc.vector.tensor_tensor(
+                scaled[:, h, :].rearrange("p (n j) -> p n j", j=PACK),
+                prob_b[h][:].rearrange("p (n j) -> p n j", j=PACK),
+                spread.rearrange("p j n -> p n j"),
+                ALU.mult,
+            )
+            nc.vector.reciprocal(inv_b[:, h, :], page_b[:, h, :])
+        inv_z = sb([P, HALVES], F32, "inv_z")
+        nc.vector.reciprocal(inv_z[:], row_sum[:])
+
+        turned_sums = banks[6][:, :P]
+        for c in range(PAGE):
+            nc.tensor.matmul(
+                turned_sums,
+                prob_a[:, c, :, :].rearrange("p h g -> p (h g)"),
+                ident[:],
+                is_transpose=True,
+                start=(c == 0),
+                stop=(c == PAGE - 1),
+            )
+
+        picked = [sb([P, I], BF16, "picked_%d" % t) for t in range(PACK)]
+        mid = I // 2
+        nc.scalar.activation(picked[0][:], windows[0][:].indirect(offsets[:]), ACT.Copy)
+        nc.scalar.activation(picked[1][:], windows[1][:].indirect(offsets[:]), ACT.Copy)
+        nc.scalar.activation(picked[2][:], windows[2][:].indirect(offsets[:]), ACT.Copy)
+
+        on_0 = sb([P, 2, P], F32, "on_0", tag="on_0")
+        nc.vector.tensor_copy(on_0[:, 0, :], turned_sums)
+        page_a = banks[2][:, :P]
+        nc.tensor.transpose(page_a, on_0[:, 0, :], ident[:])
+        ratio = on_0[:, 1, :]
+        nc.vector.tensor_tensor(ratio, page_a, inv_b[:].rearrange("p h g -> p (h g)"), ALU.mult)
+        weights = []
+        for h in range(HALVES):
+            rounded = sb([P, I], BF16, "weights_%d" % h)
+            nc.vector.scalar_tensor_tensor(
+                rounded[:].rearrange("p (g c) -> p g c", c=PAGE),
+                scaled[:, h, :].rearrange("p (g c) -> p g c", c=PAGE),
+                inv_z[:, h : h + 1],
+                ratio[:, h * G : (h + 1) * G].unsqueeze(2).to_broadcast([P, G, PAGE]),
+                ALU.mult,
+                ALU.mult,
+            )
+            weights.append(rounded)
+        nc.vector.tensor_copy(picked[3][:, :mid], windows[3][:].indirect(offsets[:, : mid // 16]))
+        nc.scalar.activation(picked[3][:, mid:], windows[3][:].indirect(offsets[:, mid // 16 :]), ACT.Copy)
+
+        def turn(rows_bf16, target):
+            words = rows_bf16.bitcast(F32)
+            for u in range(2):
+                nc.tensor.transpose(target[:, u * P : (u + 1) * P], words[:, u : 2 * P : 2], ident[:])
+
+        def weave(copy, grouped, source):
+            copy(
+                grouped.bitcast(F32).rearrange("p (n r u) -> p n r u", u=2, r=P),
+                source.rearrange("p (n u r) -> p n r u", u=2, r=P),
+            )
+
+        on_scalar, on_vector = nc.scalar.copy, nc.vector.tensor_copy
+        codes = reuse.tile([P, Q + E], U32, name="codes", offset=0, align_bytes=64)
+        late = reuse.tile([P, 4 * I], BF16, name="late", offset=4096, align_bytes=64)
+        scales = sb([P, Q + E], U8, "scales")
+        w_first = sb([P, I], BF16, "w_first")
+        v_last = sb([P, I], BF16, "v_last")
+
+        def quantize(grouped, first, count):
+            nc.vector.quantize_mx(
+                codes[:, first : first + count].bitcast(FP8X4), scales[:, first : first + count], grouped
+            )
+
+        turn(picked[0][:], banks[5][:, : 2 * P])
+        turn(picked[1][:], banks[5][:, 2 * P :])
+        turn(weights[0][:], banks[3][:, : 2 * P])
+        turn(weights[1][:], banks[7][:, : 2 * P])
+        turn(picked[2][:], banks[6][:, : 2 * P])
+        turn(picked[3][:], banks[2][:, : 2 * P])
+        weave(on_vector, w_first[:], banks[3][:, : 2 * P])
+        quantize(w_first[:], 0, P)
+        weave(on_vector, late[:, :I], banks[7][:, : 2 * P])
+        quantize(late[:, :I], P, P)
+        weave(on_scalar, late[:, I : 3 * I], banks[5][:])
+        quantize(late[:, I : 3 * I], Q, 2 * P)
+        weave(on_scalar, late[:, 3 * I :], banks[6][:, : 2 * P])
+        quantize(late[:, 3 * I :], Q + 2 * P, P)
+        weave(on_scalar, v_last[:], banks[2][:, : 2 * P])
+        quantize(v_last[:], Q + 3 * P, P)
+
+        def product(target, t, cols):
+            rows = slice(Q + t * P, Q + (t + 1) * P)
+            nc.tensor.matmul_mx(
+                target,
+                lhsT=codes[:, rows].bitcast(FP8X4),
+                lhsT_scale=scales[:, rows],
+                rhs=codes[:, cols].bitcast(FP8X4),
+                rhs_scale=scales[:, cols],
+                start=True,
+                stop=True,
+            )
+
+        out_rows = out_0.rearrange("(p j) q -> p j q", j=PACK)
+        result = sb([P, PACK, Q], F32, "result")
+        for t, bank in enumerate((banks[0], banks[1], banks[4])):
+            product(bank[:, :Q], t, slice(0, Q))
+            on_scalar(result[:, t, :], bank[:, :Q])
+        nc.sync.dma_start(out_rows[:, : PACK - 1, :], result[:, : PACK - 1, :])
+        o_codes = sb([P, Q], U32, "o_codes")
+        o_scales = sb([P, Q], U8, "o_scales")
+        for h, (bank, copy) in enumerate(((banks[3], on_vector), (banks[5], on_scalar))):
+            cols = slice(h * P, (h + 1) * P)
+            product(bank[:, :P], PACK - 1, cols)
+            copy(result[:, PACK - 1, cols], bank[:, :P])
+        nc.scalar.dma_start(out_rows[:, PACK - 1, :], result[:, PACK - 1, :])
+        for h, copy in enumerate((on_vector, on_scalar)):
+            cols = slice(h * P, (h + 1) * P)
+            grouped = sb([P, P, PACK], BF16, "o_grouped_%d" % h)
+            copy(
+                grouped[:].rearrange("p (c i) t -> p c t i", i=4),
+                result[:, :, cols].rearrange("p t (c i) -> p c t i", i=4),
+            )
+            nc.vector.quantize_mx(
+                o_codes[:, cols].bitcast(FP8X4), o_scales[:, cols], grouped[:].rearrange("p q t -> p (q t)")
+            )
+        nc.sync.dma_start(
+            out_1[0].rearrange("p c r -> p (c r)").bitcast(I32), o_codes[:].bitcast(I32)
+        )
+        for quad in range(4):
+            queue = nc.sync if quad < 2 else nc.scalar
+            queue.dma_start(
+                out_2[0, 4 * quad : 4 * quad + 4, :].bitcast(I32),
+                o_scales[32 * quad : 32 * quad + 4, :].bitcast(I32),
+            )

@@ -21,6 +21,7 @@ P = 128
 PACK = 4
 PAGE = I // G
 HALVES = Q // P
+SHARE = 36
 
 
 def tile_attend_pagethensecond_pl_kernel(
@@ -40,22 +41,22 @@ def tile_attend_pagethensecond_pl_kernel(
         offsets = keep.tile([P, I // 16], U16, name="offsets")
         nc.sync.dma_start(offsets[:], offs)
         factor = sb([P, PACK], F32, "factor")
-        nc.scalar.dma_start(factor[:], slot_factor.rearrange("o (p j) -> (o p) j", j=PACK))
+        nc.sync.dma_start(factor[:], slot_factor.rearrange("o (p j) -> (o p) j", j=PACK))
         key_bytes = sb([P, T], U8, "key_bytes")
         nc.vector.memset(key_bytes[:].bitcast(I32), 0)
-        raw_q = {name: sb([P, PACK, Q], F32, "raw_q_" + name) for name in ("b", "a")}
-        nc.sync.dma_start(raw_q["b"][:], query2.rearrange("(p j) w -> p j w", j=PACK))
+        key_words = sb([P, T], U32, "key_words")
+        words_in = keys_words[0].rearrange("p n t -> p (n t)").bitcast(I32)
+        nc.sync.dma_start(key_words[:, : T // 2].bitcast(I32), words_in[:, : T // 2])
         for quad in range(4):
             nc.sync.dma_start(
                 key_bytes[32 * quad : 32 * quad + 4, :].bitcast(I32),
                 keys_scales[0, 4 * quad : 4 * quad + 4, :].bitcast(I32),
             )
-        key_words = sb([P, T], U32, "key_words")
-        nc.sync.dma_start(
-            key_words[:].bitcast(I32),
-            keys_words[0].rearrange("p n t -> p (n t)").bitcast(I32),
-        )
-        nc.sync.dma_start(raw_q["a"][:], query.rearrange("(p j) w -> p j w", j=PACK))
+        nc.sync.dma_start(key_words[:, T // 2 :].bitcast(I32), words_in[:, T // 2 :])
+        raw_q = {}
+        for name, source in (("b", query2), ("a", query)):
+            raw_q[name] = sb([P, PACK, Q], F32, "raw_q_" + name)
+            nc.sync.dma_start(raw_q[name][:], source.rearrange("(p j) w -> p j w", j=PACK))
         pool_rows = vals.rearrange("(p j) c -> p j c", j=PACK)
         windows = []
         for t in range(PACK):
@@ -73,6 +74,11 @@ def tile_attend_pagethensecond_pl_kernel(
         for j in range(PACK):
             nc.tensor.transpose(spread[:, j, :], factor[:, j : j + 1].to_broadcast([P, P]), ident[:])
 
+        factor_row = sb([P, I], F32, "factor_row")
+        nc.scalar.copy(
+            factor_row[:].rearrange("p (n j) -> p n j", j=PACK), spread.rearrange("p j n -> p n j")
+        )
+
         k_scales = sb([P, I], U8, "k_scales")
         nc.vector.tensor_copy(k_scales[:], key_bytes[:].indirect(offsets[:]))
         k_codes = sb([P, I], U32, "k_codes")
@@ -82,11 +88,14 @@ def tile_attend_pagethensecond_pl_kernel(
         prob_a = sb([P, PAGE, HALVES, G], F32, "prob_a")
         row_sum = sb([P, HALVES], F32, "row_sum")
         for n, name in enumerate(("b", "a")):
-            grouped = sb([P, Q, PACK], BF16, "q_grouped_" + name)
-            nc.vector.tensor_copy(
-                grouped[:].rearrange("p (c i) t -> p c t i", i=4),
-                raw_q[name][:].rearrange("p t (c i) -> p c t i", i=4),
-            )
+            grouped = sb([P, Q, PACK], BF16, "q_grouped_" + name, tag="q_grouped")
+            dealt = grouped[:].rearrange("p (c i) t -> p c t i", i=4)
+            plain = raw_q[name][:].rearrange("p t (c i) -> p c t i", i=4)
+            if name == "b":
+                nc.vector.tensor_copy(dealt[:, :SHARE], plain[:, :SHARE])
+                nc.scalar.activation(dealt[:, SHARE:], plain[:, SHARE:], ACT.Copy)
+            else:
+                nc.vector.tensor_copy(dealt, plain)
             q_codes = sb([P, Q], U32, "q_codes_" + name)
             q_scales = sb([P, Q], U8, "q_scales_" + name)
             nc.vector.quantize_mx(
@@ -121,12 +130,7 @@ def tile_attend_pagethensecond_pl_kernel(
             nc.vector.tensor_reduce(
                 page_b[:, h, :], prob_b[h][:].rearrange("p (g c) -> p g c", c=PAGE), AX.X, ALU.add
             )
-            nc.vector.tensor_tensor(
-                scaled[:, h, :].rearrange("p (n j) -> p n j", j=PACK),
-                prob_b[h][:].rearrange("p (n j) -> p n j", j=PACK),
-                spread.rearrange("p j n -> p n j"),
-                ALU.mult,
-            )
+            nc.gpsimd.tensor_tensor(scaled[:, h, :], prob_b[h][:], factor_row[:], ALU.mult)
             nc.vector.reciprocal(inv_b[:, h, :], page_b[:, h, :])
         inv_z = sb([P, HALVES], F32, "inv_z")
         nc.vector.reciprocal(inv_z[:], row_sum[:])
@@ -144,11 +148,11 @@ def tile_attend_pagethensecond_pl_kernel(
 
         picked = [sb([P, I], BF16, "picked_%d" % t) for t in range(PACK)]
         mid = I // 2
-        nc.scalar.activation(picked[0][:], windows[0][:].indirect(offsets[:]), ACT.Copy)
+        nc.vector.tensor_copy(picked[0][:], windows[0][:].indirect(offsets[:]))
         nc.scalar.activation(picked[1][:], windows[1][:].indirect(offsets[:]), ACT.Copy)
         nc.scalar.activation(picked[2][:], windows[2][:].indirect(offsets[:]), ACT.Copy)
 
-        on_0 = sb([P, 2, P], F32, "on_0", tag="on_0")
+        on_0 = sb([P, 2, P], F32, "on_0", tag="vals_0")
         nc.vector.tensor_copy(on_0[:, 0, :], turned_sums)
         page_a = banks[2][:, :P]
         nc.tensor.transpose(page_a, on_0[:, 0, :], ident[:])
@@ -181,51 +185,50 @@ def tile_attend_pagethensecond_pl_kernel(
             )
 
         on_scalar, on_vector = nc.scalar.copy, nc.vector.tensor_copy
-        codes = reuse.tile([P, Q + E], U32, name="codes", offset=0, align_bytes=64)
-        late = reuse.tile([P, 4 * I], BF16, name="late", offset=4096, align_bytes=64)
-        scales = sb([P, Q + E], U8, "scales")
-        w_first = sb([P, I], BF16, "w_first")
+        late_codes = reuse.tile([P, Q + 3 * P], U32, name="late_codes", offset=0, align_bytes=64)
+        v_third = reuse.tile([P, I], BF16, name="v_third", offset=4096, align_bytes=64)
+        first_codes = sb([P, P], U32, "first_codes", tag="raw_q_a")
+        w_codes = late_codes[:, :Q]
+        v_codes = [first_codes[:]] + [late_codes[:, Q + t * P : Q + (t + 1) * P] for t in range(PACK - 1)]
+        v_scales = sb([P, PACK, P], U8, "v_scales")
+        w_scales = sb([P, Q], U8, "w_scales")
+        w_grouped = sb([P, 2 * I], BF16, "w_grouped")
+        v_first = sb([P, I], BF16, "v_first", tag="vals_1")
+        v_second = sb([P, I], BF16, "v_second", tag="vals_2")
         v_last = sb([P, I], BF16, "v_last")
 
-        def quantize(grouped, first, count):
-            nc.vector.quantize_mx(
-                codes[:, first : first + count].bitcast(FP8X4), scales[:, first : first + count], grouped
-            )
-
-        turn(picked[0][:], banks[5][:, : 2 * P])
-        turn(picked[1][:], banks[5][:, 2 * P :])
+        turn(picked[0][:], banks[6][:, : 2 * P])
+        weave(on_scalar, v_first[:], banks[6][:, : 2 * P])
+        turn(picked[1][:], banks[6][:, 2 * P :])
         turn(weights[0][:], banks[3][:, : 2 * P])
         turn(weights[1][:], banks[7][:, : 2 * P])
-        turn(picked[2][:], banks[6][:, : 2 * P])
+        turn(picked[2][:], banks[5][:, : 2 * P])
         turn(picked[3][:], banks[2][:, : 2 * P])
-        weave(on_vector, w_first[:], banks[3][:, : 2 * P])
-        quantize(w_first[:], 0, P)
-        weave(on_vector, late[:, :I], banks[7][:, : 2 * P])
-        quantize(late[:, :I], P, P)
-        weave(on_scalar, late[:, I : 3 * I], banks[5][:])
-        quantize(late[:, I : 3 * I], Q, 2 * P)
-        weave(on_scalar, late[:, 3 * I :], banks[6][:, : 2 * P])
-        quantize(late[:, 3 * I :], Q + 2 * P, P)
+        weave(on_vector, w_grouped[:, :I], banks[3][:, : 2 * P])
+        weave(on_vector, w_grouped[:, I:], banks[7][:, : 2 * P])
+        weave(on_scalar, v_second[:], banks[6][:, 2 * P :])
+        weave(on_scalar, v_third[:], banks[5][:, : 2 * P])
         weave(on_scalar, v_last[:], banks[2][:, : 2 * P])
-        quantize(v_last[:], Q + 3 * P, P)
+        nc.vector.quantize_mx(w_codes.bitcast(FP8X4), w_scales[:], w_grouped[:])
+        for t, grouped in enumerate((v_first, v_second, v_third, v_last)):
+            nc.vector.quantize_mx(v_codes[t].bitcast(FP8X4), v_scales[:, t, :], grouped[:])
 
         def product(target, t, cols):
-            rows = slice(Q + t * P, Q + (t + 1) * P)
             nc.tensor.matmul_mx(
                 target,
-                lhsT=codes[:, rows].bitcast(FP8X4),
-                lhsT_scale=scales[:, rows],
-                rhs=codes[:, cols].bitcast(FP8X4),
-                rhs_scale=scales[:, cols],
+                lhsT=v_codes[t].bitcast(FP8X4),
+                lhsT_scale=v_scales[:, t, :],
+                rhs=w_codes[:, cols].bitcast(FP8X4),
+                rhs_scale=w_scales[:, cols],
                 start=True,
                 stop=True,
             )
 
         out_rows = out_0.rearrange("(p j) q -> p j q", j=PACK)
         result = sb([P, PACK, Q], F32, "result")
-        for t, bank in enumerate((banks[0], banks[1], banks[4])):
+        for t, (bank, copy) in enumerate(((banks[0], on_vector), (banks[1], on_scalar), (banks[4], on_vector))):
             product(bank[:, :Q], t, slice(0, Q))
-            on_scalar(result[:, t, :], bank[:, :Q])
+            copy(result[:, t, :], bank[:, :Q])
         nc.sync.dma_start(out_rows[:, : PACK - 1, :], result[:, : PACK - 1, :])
         o_codes = sb([P, Q], U32, "o_codes")
         o_scales = sb([P, Q], U8, "o_scales")

@@ -185,39 +185,43 @@ def tile_attend_pagethensecond_pl_kernel(
             )
 
         on_scalar, on_vector = nc.scalar.copy, nc.vector.tensor_copy
-        late_codes = reuse.tile([P, Q + 3 * P], U32, name="late_codes", offset=0, align_bytes=64)
-        v_third = reuse.tile([P, I], BF16, name="v_third", offset=4096, align_bytes=64)
-        first_codes = sb([P, P], U32, "first_codes", tag="raw_q_a")
+        late_codes = reuse.tile([P, Q + E], U32, name="late_codes", offset=0, align_bytes=64)
+        late = reuse.tile([P, 2, I], BF16, name="late", offset=4096, align_bytes=64)
         w_codes = late_codes[:, :Q]
-        v_codes = [first_codes[:]] + [late_codes[:, Q + t * P : Q + (t + 1) * P] for t in range(PACK - 1)]
-        v_scales = sb([P, PACK, P], U8, "v_scales")
+        v_codes = late_codes[:, Q:]
+        v_scales = sb([P, E], U8, "v_scales")
         w_scales = sb([P, Q], U8, "w_scales")
-        w_grouped = sb([P, 2 * I], BF16, "w_grouped")
-        v_first = sb([P, I], BF16, "v_first", tag="vals_1")
-        v_second = sb([P, I], BF16, "v_second", tag="vals_2")
+        middle = sb([P, 3, I], BF16, "middle", tag="vals_2")
         v_last = sb([P, I], BF16, "v_last")
 
         turn(picked[0][:], banks[6][:, : 2 * P])
-        weave(on_scalar, v_first[:], banks[6][:, : 2 * P])
-        turn(picked[1][:], banks[6][:, 2 * P :])
+        turn(picked[1][:], banks[4][:, : 2 * P])
         turn(weights[0][:], banks[3][:, : 2 * P])
         turn(weights[1][:], banks[7][:, : 2 * P])
         turn(picked[2][:], banks[5][:, : 2 * P])
         turn(picked[3][:], banks[2][:, : 2 * P])
-        weave(on_vector, w_grouped[:, :I], banks[3][:, : 2 * P])
-        weave(on_vector, w_grouped[:, I:], banks[7][:, : 2 * P])
-        weave(on_scalar, v_second[:], banks[6][:, 2 * P :])
-        weave(on_scalar, v_third[:], banks[5][:, : 2 * P])
+        weave(on_vector, middle[:, 0, :], banks[6][:, : 2 * P])
+        weave(on_scalar, middle[:, 1, :], banks[4][:, : 2 * P])
+        weave(on_scalar, middle[:, 2, :], banks[3][:, : 2 * P])
+        weave(on_scalar, late[:, 0, :], banks[7][:, : 2 * P])
+        weave(on_scalar, late[:, 1, :], banks[5][:, : 2 * P])
         weave(on_scalar, v_last[:], banks[2][:, : 2 * P])
-        nc.vector.quantize_mx(w_codes.bitcast(FP8X4), w_scales[:], w_grouped[:])
-        for t, grouped in enumerate((v_first, v_second, v_third, v_last)):
-            nc.vector.quantize_mx(v_codes[t].bitcast(FP8X4), v_scales[:, t, :], grouped[:])
+
+        def quantize(codes, scales, first, count, grouped):
+            cols = slice(first * P, (first + count) * P)
+            nc.vector.quantize_mx(codes[:, cols].bitcast(FP8X4), scales[:, cols], grouped)
+
+        quantize(w_codes, w_scales, 0, 1, middle[:, 2, :])
+        quantize(v_codes, v_scales, 0, 2, middle[:, :2, :].rearrange("p t i -> p (t i)"))
+        quantize(w_codes, w_scales, 1, 1, late[:, 0, :])
+        quantize(v_codes, v_scales, 2, 1, late[:, 1, :])
+        quantize(v_codes, v_scales, 3, 1, v_last[:])
 
         def product(target, t, cols):
             nc.tensor.matmul_mx(
                 target,
-                lhsT=v_codes[t].bitcast(FP8X4),
-                lhsT_scale=v_scales[:, t, :],
+                lhsT=v_codes[:, t * P : (t + 1) * P].bitcast(FP8X4),
+                lhsT_scale=v_scales[:, t * P : (t + 1) * P],
                 rhs=w_codes[:, cols].bitcast(FP8X4),
                 rhs_scale=w_scales[:, cols],
                 start=True,
@@ -226,7 +230,7 @@ def tile_attend_pagethensecond_pl_kernel(
 
         out_rows = out_0.rearrange("(p j) q -> p j q", j=PACK)
         result = sb([P, PACK, Q], F32, "result")
-        for t, (bank, copy) in enumerate(((banks[0], on_vector), (banks[1], on_scalar), (banks[4], on_vector))):
+        for t, (bank, copy) in enumerate(((banks[0], on_scalar), (banks[1], on_vector), (banks[4], on_scalar))):
             product(bank[:, :Q], t, slice(0, Q))
             copy(result[:, t, :], bank[:, :Q])
         nc.sync.dma_start(out_rows[:, : PACK - 1, :], result[:, : PACK - 1, :])
@@ -236,7 +240,7 @@ def tile_attend_pagethensecond_pl_kernel(
             cols = slice(h * P, (h + 1) * P)
             product(bank[:, :P], PACK - 1, cols)
             copy(result[:, PACK - 1, cols], bank[:, :P])
-        nc.scalar.dma_start(out_rows[:, PACK - 1, :], result[:, PACK - 1, :])
+        nc.sync.dma_start(out_rows[:, PACK - 1, :], result[:, PACK - 1, :])
         for h, copy in enumerate((on_vector, on_scalar)):
             cols = slice(h * P, (h + 1) * P)
             grouped = sb([P, P, PACK], BF16, "o_grouped_%d" % h)

@@ -39,18 +39,18 @@ def tile_attend_pagethensecond_pl_kernel(
         banks = [psum.tile([P, I], F32, name="bank_%d" % n) for n in range(8)]
 
         offsets = keep.tile([P, I // 16], U16, name="offsets")
+        key_words = sb([P, T], U32, "key_words")
+        words_in = keys_words[0].rearrange("p n t -> p (n t)").bitcast(I32)
+        nc.sync.dma_start(key_words[:, : T // 2].bitcast(I32), words_in[:, : T // 2])
         nc.sync.dma_start(offsets[:], offs)
         factor = sb([P, PACK], F32, "factor")
         nc.sync.dma_start(factor[:], slot_factor.rearrange("o (p j) -> (o p) j", j=PACK))
         key_bytes = sb([P, T], U8, "key_bytes")
         nc.vector.memset(key_bytes[:].bitcast(I32), 0)
-        key_words = sb([P, T], U32, "key_words")
-        words_in = keys_words[0].rearrange("p n t -> p (n t)").bitcast(I32)
-        nc.sync.dma_start(key_words[:, : T // 2].bitcast(I32), words_in[:, : T // 2])
-        for quad in range(4):
+        for row in range(4):
             nc.sync.dma_start(
-                key_bytes[32 * quad : 32 * quad + 4, :].bitcast(I32),
-                keys_scales[0, 4 * quad : 4 * quad + 4, :].bitcast(I32),
+                key_bytes[row:P:32, :].bitcast(I32),
+                keys_scales[0, row:16:4, :].bitcast(I32),
             )
         nc.sync.dma_start(key_words[:, T // 2 :].bitcast(I32), words_in[:, T // 2 :])
         raw_q = {}
@@ -233,14 +233,14 @@ def tile_attend_pagethensecond_pl_kernel(
         for t, (bank, copy) in enumerate(((banks[0], on_scalar), (banks[1], on_vector), (banks[4], on_scalar))):
             product(bank[:, :Q], t, slice(0, Q))
             copy(result[:, t, :], bank[:, :Q])
-        nc.sync.dma_start(out_rows[:, : PACK - 1, :], result[:, : PACK - 1, :])
+        nc.sync.dma_start(out_rows[:, :2, :], result[:, :2, :])
         o_codes = sb([P, Q], U32, "o_codes")
         o_scales = sb([P, Q], U8, "o_scales")
         for h, (bank, copy) in enumerate(((banks[3], on_vector), (banks[5], on_scalar))):
             cols = slice(h * P, (h + 1) * P)
             product(bank[:, :P], PACK - 1, cols)
             copy(result[:, PACK - 1, cols], bank[:, :P])
-        nc.sync.dma_start(out_rows[:, PACK - 1, :], result[:, PACK - 1, :])
+        nc.sync.dma_start(out_rows[:, 2:, :], result[:, 2:, :])
         for h, copy in enumerate((on_vector, on_scalar)):
             cols = slice(h * P, (h + 1) * P)
             grouped = sb([P, P, PACK], BF16, "o_grouped_%d" % h)

@@ -41,12 +41,12 @@ def tile_attend_pagethensecond_pl_kernel(
         offsets = keep.tile([P, I // 16], U16, name="offsets")
         key_words = sb([P, T], U32, "key_words")
         words_in = keys_words[0].rearrange("p n t -> p (n t)").bitcast(I32)
-        nc.sync.dma_start(key_words[:, : T // 2].bitcast(I32), words_in[:, : T // 2])
         nc.sync.dma_start(offsets[:], offs)
         factor = sb([P, PACK], F32, "factor")
         nc.sync.dma_start(factor[:], slot_factor.rearrange("o (p j) -> (o p) j", j=PACK))
         key_bytes = sb([P, T], U8, "key_bytes")
         nc.vector.memset(key_bytes[:].bitcast(I32), 0)
+        nc.sync.dma_start(key_words[:, : T // 2].bitcast(I32), words_in[:, : T // 2])
         for row in range(4):
             nc.sync.dma_start(
                 key_bytes[row:P:32, :].bitcast(I32),
@@ -157,16 +157,18 @@ def tile_attend_pagethensecond_pl_kernel(
         page_a = banks[2][:, :P]
         nc.tensor.transpose(page_a, on_0[:, 0, :], ident[:])
         ratio = on_0[:, 1, :]
-        nc.vector.tensor_tensor(ratio, page_a, inv_b[:].rearrange("p h g -> p (h g)"), ALU.mult)
+        for h in range(HALVES):
+            pages = slice(h * G, (h + 1) * G)
+            nc.vector.scalar_tensor_tensor(
+                ratio[:, pages], page_a[:, pages], inv_z[:, h : h + 1], inv_b[:, h, :], ALU.mult, ALU.mult
+            )
         weights = []
         for h in range(HALVES):
             rounded = sb([P, I], BF16, "weights_%d" % h)
-            nc.vector.scalar_tensor_tensor(
+            nc.vector.tensor_tensor(
                 rounded[:].rearrange("p (g c) -> p g c", c=PAGE),
                 scaled[:, h, :].rearrange("p (g c) -> p g c", c=PAGE),
-                inv_z[:, h : h + 1],
                 ratio[:, h * G : (h + 1) * G].unsqueeze(2).to_broadcast([P, G, PAGE]),
-                ALU.mult,
                 ALU.mult,
             )
             weights.append(rounded)

from contextlib import ExitStack

import concourse.mybir as mybir
from concourse.masks import make_identity

D, E, T, I, Q, G = 512, 512, 2048, 512, 256, 64
FLOPS = 2 * (2 * D * Q * I) + 2 * I * E * Q

F32 = mybir.dt.float32
BF16 = mybir.dt.bfloat16
I32 = mybir.dt.int32
U32 = mybir.dt.uint32
U16 = mybir.dt.uint16
U8 = mybir.dt.uint8
FP8X4 = mybir.dt.float8_e4m3fn_x4
ALU = mybir.AluOpType
ACT = mybir.ActivationFunctionType
AX = mybir.AxisListType

P = 128
PACK = 4
PAGE = I // G
HALVES = Q // P
SHARE = 36


def tile_attend_pagethensecond_pl_kernel(
    tc, query, query2, keys_words, keys_scales, slot_factor, vals, offs, out_0, out_1, out_2
):
    nc = tc.nc
    with ExitStack() as ctx:
        keep = ctx.enter_context(tc.tile_pool(name="keep", bufs=1))
        reuse = ctx.enter_context(tc.tile_pool(name="reuse", bufs=1))
        psum = ctx.enter_context(tc.psum_pool(name="psum", bufs=1))

        def sb(shape, dtype, name, tag=None):
            return keep.tile(shape, dtype, name=name, tag=tag or name, align_bytes=64)

        banks = [psum.tile([P, I], F32, name="bank_%d" % n) for n in range(8)]

        offsets = keep.tile([P, I // 16], U16, name="offsets")
        key_words = sb([P, T], U32, "key_words")
        words_in = keys_words[0].rearrange("p n t -> p (n t)").bitcast(I32)
        nc.sync.dma_start(offsets[:], offs)
        factor = sb([P, PACK], F32, "factor")
        nc.sync.dma_start(factor[:], slot_factor.rearrange("o (p j) -> (o p) j", j=PACK))
        key_bytes = sb([P, T], U8, "key_bytes")
        nc.vector.memset(key_bytes[:].bitcast(I32), 0)
        nc.sync.dma_start(key_words[:, : T // 2].bitcast(I32), words_in[:, : T // 2])
        for row in range(4):
            nc.sync.dma_start(
                key_bytes[row:P:32, :].bitcast(I32),
                keys_scales[0, row:16:4, :].bitcast(I32),
            )
        nc.sync.dma_start(key_words[:, T // 2 :].bitcast(I32), words_in[:, T // 2 :])
        raw_q = {}
        for name, source in (("b", query2), ("a", query)):
            raw_q[name] = sb([P, PACK, Q], F32, "raw_q_" + name)
            nc.sync.dma_start(raw_q[name][:], source.rearrange("(p j) w -> p j w", j=PACK))
        pool_rows = vals.rearrange("(p j) c -> p j c", j=PACK)
        windows = []
        for t in range(PACK):
            if t < PACK - 1:
                window = sb([P, T], F32, "vals_%d" % t)
            else:
                window = reuse.tile([P, T], F32, name="vals_last", offset=0, align_bytes=64)
            nc.sync.dma_start(window[:], pool_rows[:, t, :])
            windows.append(window)

        ident = sb([P, P], F32, "ident")
        make_identity(nc, ident[:])

        spread = banks[4][:].rearrange("p (j n) -> p j n", j=PACK)
        for j in range(PACK):
            nc.tensor.transpose(spread[:, j, :], factor[:, j : j + 1].to_broadcast([P, P]), ident[:])

        factor_row = sb([P, I], F32, "factor_row")
        nc.scalar.copy(
            factor_row[:].rearrange("p (n j) -> p n j", j=PACK), spread.rearrange("p j n -> p n j")
        )

        k_scales = sb([P, I], U8, "k_scales")
        nc.vector.tensor_copy(k_scales[:], key_bytes[:].indirect(offsets[:]))
        k_codes = sb([P, I], U32, "k_codes")
        nc.vector.tensor_copy(k_codes[:], key_words[:].indirect(offsets[:]))

        prob_b = [sb([P, I], F32, "prob_b_%d" % h) for h in range(HALVES)]
        prob_a = sb([P, PAGE, HALVES, G], F32, "prob_a")
        row_sum = sb([P, HALVES], F32, "row_sum")
        for n, name in enumerate(("b", "a")):
            grouped = sb([P, Q, PACK], BF16, "q_grouped_" + name, tag="q_grouped")
            dealt = grouped[:].rearrange("p (c i) t -> p c t i", i=4)
            plain = raw_q[name][:].rearrange("p t (c i) -> p c t i", i=4)
            if name == "b":
                nc.vector.tensor_copy(dealt[:, :SHARE], plain[:, :SHARE])
                nc.scalar.activation(dealt[:, SHARE:], plain[:, SHARE:], ACT.Copy)
            else:
                nc.vector.tensor_copy(dealt, plain)
            q_codes = sb([P, Q], U32, "q_codes_" + name)
            q_scales = sb([P, Q], U8, "q_scales_" + name)
            nc.vector.quantize_mx(
                q_codes[:].bitcast(FP8X4), q_scales[:], grouped[:].rearrange("p w t -> p (w t)")
            )
            for h in range(HALVES):
                cols = slice(h * P, (h + 1) * P)
                scores = banks[HALVES * n + h]
                nc.tensor.matmul_mx(
                    scores[:],
                    lhsT=q_codes[:, cols].bitcast(FP8X4),
                    lhsT_scale=q_scales[:, cols],
                    rhs=k_codes[:].bitcast(FP8X4),
                    rhs_scale=k_scales[:],
                    start=True,
                    stop=True,
                )
                if name == "a":
                    nc.scalar.activation(
                        prob_a[:, :, h, :],
                        scores[:].rearrange("p (g c) -> p c g", c=PAGE),
                        ACT.Exp,
                        accum_out=row_sum[:, h : h + 1],
                    )
                else:
                    nc.scalar.activation(prob_b[h][:], scores[:], ACT.Exp)

        page_b = sb([P, HALVES, G], F32, "page_b")
        inv_b = sb([P, HALVES, G], F32, "inv_b")
        scaled = sb([P, HALVES, I], F32, "scaled", tag="raw_q_a")
        for h in range(HALVES):
            nc.vector.tensor_reduce(
                page_b[:, h, :], prob_b[h][:].rearrange("p (g c) -> p g c", c=PAGE), AX.X, ALU.add
            )
            nc.gpsimd.tensor_tensor(scaled[:, h, :], prob_b[h][:], factor_row[:], ALU.mult)
            nc.vector.reciprocal(inv_b[:, h, :], page_b[:, h, :])
        inv_z = sb([P, HALVES], F32, "inv_z")
        nc.vector.reciprocal(inv_z[:], row_sum[:])

        turned_sums = banks[6][:, :P]
        for c in range(PAGE):
            nc.tensor.matmul(
                turned_sums,
                prob_a[:, c, :, :].rearrange("p h g -> p (h g)"),
                ident[:],
                is_transpose=True,
                start=(c == 0),
                stop=(c == PAGE - 1),
            )

        picked = [sb([P, I], BF16, "picked_%d" % t) for t in range(PACK)]
        mid = I // 2
        nc.vector.tensor_copy(picked[0][:], windows[0][:].indirect(offsets[:]))
        nc.scalar.activation(picked[1][:], windows[1][:].indirect(offsets[:]), ACT.Copy)
        nc.scalar.activation(picked[2][:], windows[2][:].indirect(offsets[:]), ACT.Copy)

        on_0 = sb([P, 2, P], F32, "on_0", tag="vals_0")
        nc.vector.tensor_copy(on_0[:, 0, :], turned_sums)
        page_a = banks[2][:, :P]
        nc.tensor.transpose(page_a, on_0[:, 0, :], ident[:])
        ratio = on_0[:, 1, :]
        for h in range(HALVES):
            pages = slice(h * G, (h + 1) * G)
            nc.vector.scalar_tensor_tensor(
                ratio[:, pages], page_a[:, pages], inv_z[:, h : h + 1], inv_b[:, h, :], ALU.mult, ALU.mult
            )
        weights = []
        for h in range(HALVES):
            rounded = sb([P, I], BF16, "weights_%d" % h)
            nc.vector.tensor_tensor(
                rounded[:].rearrange("p (g c) -> p g c", c=PAGE),
                scaled[:, h, :].rearrange("p (g c) -> p g c", c=PAGE),
                ratio[:, h * G : (h + 1) * G].unsqueeze(2).to_broadcast([P, G, PAGE]),
                ALU.mult,
            )
            weights.append(rounded)
        nc.vector.tensor_copy(picked[3][:, :mid], windows[3][:].indirect(offsets[:, : mid // 16]))
        nc.scalar.activation(picked[3][:, mid:], windows[3][:].indirect(offsets[:, mid // 16 :]), ACT.Copy)

        def turn(rows_bf16, target):
            words = rows_bf16.bitcast(F32)
            for u in range(2):
                nc.tensor.transpose(target[:, u * P : (u + 1) * P], words[:, u : 2 * P : 2], ident[:])

        def weave(copy, grouped, source):
            copy(
                grouped.bitcast(F32).rearrange("p (n r u) -> p n r u", u=2, r=P),
                source.rearrange("p (n u r) -> p n r u", u=2, r=P),
            )

        on_scalar, on_vector = nc.scalar.copy, nc.vector.tensor_copy
        late_codes = reuse.tile([P, Q + E], U32, name="late_codes", offset=0, align_bytes=64)
        late = reuse.tile([P, 2, I], BF16, name="late", offset=4096, align_bytes=64)
        w_codes = late_codes[:, :Q]
        v_codes = late_codes[:, Q:]
        v_scales = sb([P, E], U8, "v_scales")
        w_scales = sb([P, Q], U8, "w_scales")
        middle = sb([P, 3, I], BF16, "middle", tag="vals_2")
        v_last = sb([P, I], BF16, "v_last")

        turn(picked[0][:], banks[6][:, : 2 * P])
        turn(picked[1][:], banks[4][:, : 2 * P])
        turn(weights[0][:], banks[3][:, : 2 * P])
        turn(weights[1][:], banks[7][:, : 2 * P])
        turn(picked[2][:], banks[5][:, : 2 * P])
        turn(picked[3][:], banks[2][:, : 2 * P])
        weave(on_vector, middle[:, 0, :], banks[6][:, : 2 * P])
        weave(on_scalar, middle[:, 1, :], banks[4][:, : 2 * P])
        weave(on_scalar, middle[:, 2, :], banks[3][:, : 2 * P])
        weave(on_scalar, late[:, 0, :], banks[7][:, : 2 * P])
        weave(on_scalar, late[:, 1, :], banks[5][:, : 2 * P])
        weave(on_scalar, v_last[:], banks[2][:, : 2 * P])

        def quantize(codes, scales, first, count, grouped):
            cols = slice(first * P, (first + count) * P)
            nc.vector.quantize_mx(codes[:, cols].bitcast(FP8X4), scales[:, cols], grouped)

        quantize(w_codes, w_scales, 0, 1, middle[:, 2, :])
        quantize(v_codes, v_scales, 0, 2, middle[:, :2, :].rearrange("p t i -> p (t i)"))
        quantize(w_codes, w_scales, 1, 1, late[:, 0, :])
        quantize(v_codes, v_scales, 2, 1, late[:, 1, :])
        quantize(v_codes, v_scales, 3, 1, v_last[:])

        def product(target, t, cols):
            nc.tensor.matmul_mx(
                target,
                lhsT=v_codes[:, t * P : (t + 1) * P].bitcast(FP8X4),
                lhsT_scale=v_scales[:, t * P : (t + 1) * P],
                rhs=w_codes[:, cols].bitcast(FP8X4),
                rhs_scale=w_scales[:, cols],
                start=True,
                stop=True,
            )

        out_rows = out_0.rearrange("(p j) q -> p j q", j=PACK)
        result = sb([P, PACK, Q], F32, "result")
        for t, (bank, copy) in enumerate(((banks[0], on_scalar), (banks[1], on_vector), (banks[4], on_scalar))):
            product(bank[:, :Q], t, slice(0, Q))
            copy(result[:, t, :], bank[:, :Q])
        nc.sync.dma_start(out_rows[:, :2, :], result[:, :2, :])
        o_codes = sb([P, Q], U32, "o_codes")
        o_scales = sb([P, Q], U8, "o_scales")
        for h, (bank, copy) in enumerate(((banks[3], on_vector), (banks[5], on_scalar))):
            cols = slice(h * P, (h + 1) * P)
            product(bank[:, :P], PACK - 1, cols)
            copy(result[:, PACK - 1, cols], bank[:, :P])
        nc.sync.dma_start(out_rows[:, 2:, :], result[:, 2:, :])
        for h, copy in enumerate((on_vector, on_scalar)):
            cols = slice(h * P, (h + 1) * P)
            grouped = sb([P, P, PACK], BF16, "o_grouped_%d" % h)
            copy(
                grouped[:].rearrange("p (c i) t -> p c t i", i=4),
                result[:, :, cols].rearrange("p t (c i) -> p c t i", i=4),
            )
            nc.vector.quantize_mx(
                o_codes[:, cols].bitcast(FP8X4), o_scales[:, cols], grouped[:].rearrange("p q t -> p (q t)")
            )
        nc.sync.dma_start(
            out_1[0].rearrange("p c r -> p (c r)").bitcast(I32), o_codes[:].bitcast(I32)
        )
        for quad in range(4):
            queue = nc.sync if quad < 2 else nc.scalar
            queue.dma_start(
                out_2[0, 4 * quad : 4 * quad + 4, :].bitcast(I32),
                o_scales[32 * quad : 32 * quad + 4, :].bitcast(I32),
            )
